import numpy as np, ml_dtypes
CORES = [10,34,74,98]
N = 4
W, KW = 512, 5
H = KW // 2
def setup_inputs(rng):
    return {"x": rng.standard_normal((N, 128, W), dtype=np.float32).astype(ml_dtypes.bfloat16), "t": rng.standard_normal((N, 128, KW * W), dtype=np.float32).astype(ml_dtypes.bfloat16)}
def setup_inputs_big(rng):
    d = setup_inputs(rng)
    for k in ("x", "t"): d[k] = (d[k].astype(np.float32) * 1024.0).astype(d[k].dtype)
    return d
def setup_inputs_small(rng):
    d = setup_inputs(rng)
    for k in ("x", "t"): d[k] = (d[k].astype(np.float32) * (1 / 1024.0)).astype(d[k].dtype)
    return d
def reference(x, t):
    X, T = x.astype(np.float64), t.astype(np.float64)
    g = np.concatenate(list(X), axis=1)
    p = np.concatenate([g[:, -H:], g, g[:, :H]], axis=1)
    y = np.stack([sum(T[r][:, W * i:W * i + W] * p[:, W * r + i:W * r + i + W] for i in range(KW)) for r in range(N)])
    return {"y": y.astype(ml_dtypes.bfloat16 if x.dtype != np.float64 else np.float64)}

@@ -1,0 +1,113 @@
+from concourse.bass import DstId, RemoteDMATransfer
+from concourse.mybir import AluOpType
+
+W = 512
+KW = 5
+H = 2
+ORDER = [3, 4, 0, 1, 2]
+OFF = {tab: W * k for k, tab in enumerate(ORDER)}
+ENGINES_A_TRANSFER = 4
+
+SCRATCH = {
+    "acc": ("psum", [128, W], "float32"),
+    "xp": ("psum", [128, 2 * W], "float32"),
+    "xs": ("sbuf", [128, W], "bfloat16"),
+    "ts": ("sbuf", [128, KW * W], "bfloat16"),
+    "pr": ("sbuf", [128, KW * W], "bfloat16"),
+    "ys": ("sbuf", [128, W], "bfloat16"),
+    "halo": ("sbuf", [128, 2 * H], "bfloat16"),
+    "hp": ("sbuf", [128, 2 * H], "float32"),
+    "hq": ("sbuf", [128, 2], "float32"),
+    "seed": ("sbuf", [128, 128], "bfloat16"),
+    "ident": ("sbuf", [128, 128], "bfloat16"),
+    "dg": ("dram", [1, 127 * 128], "bfloat16"),
+}
+SEMAPHORES = ["xl", "c1", "c2", "m0", "ms", "xz", "d1", "idl", "p0", "p1", "p2", "p3", "p4", "accd", "yadd",
+              "arrived", "sent", "h1", "h2", "fin", "st"]
+
+
+def _bits(mask):
+    return [b for b in range(16) if (mask >> b) & 1]
+
+
+def rank_program(g, core, T, topo):
+    rank = T.rank_of(core)
+    if rank is None:
+        return
+    n = len(T.cores)
+    left, right = T.cores[(rank - 1) % n], T.cores[(rank + 1) % n]
+    S = T.sem
+    v, te, sy, sc = g.vector, g.tensor, g.sync, g.scalar
+    mult, add = AluOpType.mult, AluOpType.add
+
+    sy.dma_start(T.xs[:, :], T.x[:, :]).then_inc(S.xl, 16)
+
+    v.memset(T.ident[:, 127:128], 1.0).then_inc(S.m0, 1)
+    v.memset(T.seed[0:127, 0:1], 1.0).then_inc(S.ms, 1)
+    v.memset(T.seed[0:127, 1:128], 0.0).then_inc(S.ms, 1)
+    v.wait_ge(S.m0, 1)
+    v.memset(T.ident[0:127, 127:128], 0.0).then_inc(S.ms, 1)
+    v.memset(T.xp[:, 0:H], 0.0).then_inc(S.xz, 1)
+    v.memset(T.xp[:, H + W:H + W + H], 0.0).then_inc(S.xz, 1)
+
+    sc.wait_ge(S.ms, 3)
+    sc.dma_start(T.dg[0], T.seed[0:127, :]).then_inc(S.d1, 16)
+    sc.dma_start(T.ts[:, 0:2 * W], T.t[:, 3 * W:5 * W]).then_inc(S.c1, 16)
+    sc.dma_start(T.ts[:, 2 * W:5 * W], T.t[:, 0:3 * W]).then_inc(S.c2, 16)
+    sy.wait_ge(S.d1, 16)
+    sy.dma_start(T.ident[:, 0:127], T.dg[0]).then_inc(S.idl, 16)
+
+    for dst in (left, right):
+        if not topo.may_write(core, dst):
+            raise ValueError("core %d may not write to core %d" % (core, dst))
+    eng = [b for b in _bits(topo.mask(core, left)) if b in _bits(topo.mask(core, right))]
+    k = ENGINES_A_TRANSFER
+    m_l = sum(1 << b for b in eng[0:k])
+    m_r = sum(1 << b for b in eng[k:2 * k])
+    rid_l, pid_l = topo.addr(left)[0:2]
+    rid_r, pid_r = topo.addr(right)[0:2]
+    g.wait_ge(S.xl, 16)
+    g.remote_dma_fused([
+        RemoteDMATransfer(dst_ids=[DstId(rid=rid_l, pnc=pid_l)], dma_engine_mask=m_l, remote_sem=S.arrived,
+                          src=T.xs[:, 0:H], dst=T.halo[:, 0:H]),
+        RemoteDMATransfer(dst_ids=[DstId(rid=rid_r, pnc=pid_r)], dma_engine_mask=m_r, remote_sem=S.arrived,
+                          src=T.xs[:, W - H:W], dst=T.halo[:, H:2 * H]),
+    ], local_sem=S.sent)
+    g.wait_ge(S.sent, 2 * k)
+
+    v.wait_ge(S.xl, 16)
+    v.tensor_copy(T.xp[:, H:H + W], T.xs[:, :]).then_inc(S.xz, 1)
+    v.wait_ge(S.xz, 3)
+    for j, tab in enumerate(ORDER):
+        if j == 0:
+            v.wait_ge(S.c1, 16)
+        if j == 2:
+            v.wait_ge(S.c2, 16)
+        v.tensor_tensor(T.pr[:, W * j:W * j + W], T.ts[:, OFF[tab]:OFF[tab] + W], T.xp[:, tab:tab + W],
+                        mult).then_inc(S["p%d" % j], 1)
+
+    te.wait_ge(S.idl, 16)
+    for j in range(KW - 1):
+        te.wait_ge(S["p%d" % j], 1)
+        mm = te.matmul(T.acc[:, :], T.ident[:, :], T.pr[:, W * j:W * j + W], j == 0, j == KW - 2)
+    mm.then_inc(S.accd, 1)
+
+    v.wait_ge(S.p4, 1)
+    v.wait_ge(S.accd, 1)
+    v.tensor_tensor(T.ys[:, :], T.acc[:, :], T.pr[:, W * (KW - 1):W * KW], add).then_inc(S.yadd, 1)
+
+    v.wait_ge(S.arrived, 2 * k)
+    a = OFF[4] + W - H
+    v.tensor_tensor(T.hp[:, :], T.ts[:, a:a + 2 * H], T.halo[:, :], mult).then_inc(S.h1, 1)
+    b0, b1 = OFF[3] + W - 1, OFF[1]
+    v.tensor_tensor(T.hq[:, :], T.ts[:, b0:b1 + 1:b1 - b0], T.halo[:, 0:2 * H:2 * H - 1], mult).then_inc(S.h1, 1)
+    v.wait_ge(S.h1, 2)
+    v.tensor_tensor(T.hp[:, 1:3], T.hp[:, 1:3], T.hq[:, :], add).then_inc(S.h2, 1)
+    v.wait_ge(S.h2, 1)
+    v.wait_ge(S.yadd, 1)
+    v.tensor_tensor(T.ys[:, W - H:W], T.ys[:, W - H:W], T.hp[:, 0:H], add).then_inc(S.fin, 1)
+    v.tensor_tensor(T.ys[:, 0:H], T.ys[:, 0:H], T.hp[:, H:2 * H], add).then_inc(S.fin, 1)
+
+    sy.wait_ge(S.fin, 2)
+    sy.dma_start(T.y[:, :], T.ys[:, :]).then_inc(S.st, 16)
+    sy.wait_ge(S.st, 16)

@@ -1,29 +1,38 @@
 from concourse.bass import DstId, RemoteDMATransfer
-from concourse.mybir import AluOpType
+from concourse.mybir import AluOpType, ActivationFunctionType
 
 W = 512
 KW = 5
 H = 2
-ORDER = [3, 4, 0, 1, 2]
-OFF = {tab: W * k for k, tab in enumerate(ORDER)}
+B = 128
+NB = W // B
+XO = 256
+TABS = [2, 1, 3, 0, 4]
 ENGINES_A_TRANSFER = 4
+PIECES = [(tab, b) for tab in TABS for b in range(NB)]
 
 SCRATCH = {
-    "acc": ("psum", [128, W], "float32"),
+    "acc": ("psum", [128, NB * W], "float32"),
     "xp": ("psum", [128, 2 * W], "float32"),
     "xs": ("sbuf", [128, W], "bfloat16"),
     "ts": ("sbuf", [128, KW * W], "bfloat16"),
     "pr": ("sbuf", [128, KW * W], "bfloat16"),
     "ys": ("sbuf", [128, W], "bfloat16"),
-    "halo": ("sbuf", [128, 2 * H], "bfloat16"),
-    "hp": ("sbuf", [128, 2 * H], "float32"),
-    "hq": ("sbuf", [128, 2], "float32"),
-    "seed": ("sbuf", [128, 128], "bfloat16"),
+    "el": ("sbuf", [128, 8], "bfloat16"),
+    "er": ("sbuf", [128, 8], "bfloat16"),
+    "hr": ("sbuf", [128, 8], "bfloat16"),
+    "hl": ("sbuf", [128, 8], "bfloat16"),
+    "qr": ("sbuf", [128, 8], "bfloat16"),
+    "ql": ("sbuf", [128, 8], "bfloat16"),
+    "yer": ("sbuf", [128, 8], "bfloat16"),
+    "yel": ("sbuf", [128, 8], "bfloat16"),
+    "ones": ("sbuf", [128, 128], "bfloat16"),
     "ident": ("sbuf", [128, 128], "bfloat16"),
-    "dg": ("dram", [1, 127 * 128], "bfloat16"),
 }
-SEMAPHORES = ["xl", "c1", "c2", "m0", "ms", "xz", "d1", "idl", "p0", "p1", "p2", "p3", "p4", "accd", "yadd",
-              "arrived", "sent", "h1", "h2", "fin", "st"]
+SEMAPHORES = (["ea", "eb", "xl", "on", "xz", "idl", "xa", "xb", "arr_r", "arr_l", "sent", "yadd", "st", "st2",
+               "r1", "l1", "fr", "fl"]
+              + ["tl%d" % i for i in range(KW)] + ["p%d" % j for j in range(len(PIECES))]
+              + ["a%d" % b for b in range(NB)] + ["e%d" % b for b in range(NB - 1)])
 
 
 def _bits(mask):
@@ -39,23 +48,19 @@ def rank_program(g, core, T, topo):
     S = T.sem
     v, te, sy, sc = g.vector, g.tensor, g.sync, g.scalar
     mult, add = AluOpType.mult, AluOpType.add
+    copy = ActivationFunctionType.Copy
 
+    sy.dma_start(T.el[:, 0:H], T.x[:, 0:H]).then_inc(S.ea, 16)
+    sy.dma_start(T.er[:, 0:H], T.x[:, W - H:W]).then_inc(S.eb, 16)
     sy.dma_start(T.xs[:, :], T.x[:, :]).then_inc(S.xl, 16)
+    for tab in TABS:
+        sy.dma_start(T.ts[:, W * tab:W * tab + W], T.t[:, W * tab:W * tab + W]).then_inc(S["tl%d" % tab], 16)
 
-    v.memset(T.ident[:, 127:128], 1.0).then_inc(S.m0, 1)
-    v.memset(T.seed[0:127, 0:1], 1.0).then_inc(S.ms, 1)
-    v.memset(T.seed[0:127, 1:128], 0.0).then_inc(S.ms, 1)
-    v.wait_ge(S.m0, 1)
-    v.memset(T.ident[0:127, 127:128], 0.0).then_inc(S.ms, 1)
-    v.memset(T.xp[:, 0:H], 0.0).then_inc(S.xz, 1)
-    v.memset(T.xp[:, H + W:H + W + H], 0.0).then_inc(S.xz, 1)
-
-    sc.wait_ge(S.ms, 3)
-    sc.dma_start(T.dg[0], T.seed[0:127, :]).then_inc(S.d1, 16)
-    sc.dma_start(T.ts[:, 0:2 * W], T.t[:, 3 * W:5 * W]).then_inc(S.c1, 16)
-    sc.dma_start(T.ts[:, 2 * W:5 * W], T.t[:, 0:3 * W]).then_inc(S.c2, 16)
-    sy.wait_ge(S.d1, 16)
-    sy.dma_start(T.ident[:, 0:127], T.dg[0]).then_inc(S.idl, 16)
+    v.memset(T.ones[:, :], 1.0).then_inc(S.on, 1)
+    v.memset(T.xp[:, XO - H:XO], 0.0).then_inc(S.xz, 1)
+    v.memset(T.xp[:, XO + W:XO + W + H], 0.0).then_inc(S.xz, 1)
+    g.wait_ge(S.on, 1)
+    g.affine_select(T.ident[:, :], T.ones[:, :], [[-1, 128]], AluOpType.is_equal, 0.0, 0, 1).then_inc(S.idl, 1)
 
     for dst in (left, right):
         if not topo.may_write(core, dst):
@@ -66,48 +71,93 @@ def rank_program(g, core, T, topo):
     m_r = sum(1 << b for b in eng[k:2 * k])
     rid_l, pid_l = topo.addr(left)[0:2]
     rid_r, pid_r = topo.addr(right)[0:2]
-    g.wait_ge(S.xl, 16)
+    g.wait_ge(S.ea, 16)
     g.remote_dma_fused([
-        RemoteDMATransfer(dst_ids=[DstId(rid=rid_l, pnc=pid_l)], dma_engine_mask=m_l, remote_sem=S.arrived,
-                          src=T.xs[:, 0:H], dst=T.halo[:, 0:H]),
-        RemoteDMATransfer(dst_ids=[DstId(rid=rid_r, pnc=pid_r)], dma_engine_mask=m_r, remote_sem=S.arrived,
-                          src=T.xs[:, W - H:W], dst=T.halo[:, H:2 * H]),
+        RemoteDMATransfer(dst_ids=[DstId(rid=rid_l, pnc=pid_l)], dma_engine_mask=m_l, remote_sem=S.arr_r,
+                          src=T.el[:, 0:H], dst=T.hr[:, 0:H]),
+    ], local_sem=S.sent)
+    g.wait_ge(S.eb, 16)
+    g.remote_dma_fused([
+        RemoteDMATransfer(dst_ids=[DstId(rid=rid_r, pnc=pid_r)], dma_engine_mask=m_r, remote_sem=S.arr_l,
+                          src=T.er[:, 0:H], dst=T.hl[:, 0:H]),
     ], local_sem=S.sent)
     g.wait_ge(S.sent, 2 * k)
 
+    te.wait_ge(S.idl, 1)
+    te.wait_ge(S.xz, 2)
+    te.wait_ge(S.xl, 16)
+    te.matmul(T.xp[:, XO:XO + W // 2], T.ident[:, :], T.xs[:, 0:W // 2], True, True).then_inc(S.xa, 1)
+    sc.wait_ge(S.xz, 2)
+    sc.wait_ge(S.xl, 16)
+    sc.activation(T.xp[:, XO + W // 2:XO + W], T.xs[:, W // 2:W], copy).then_inc(S.xb, 1)
+
+    last = len(PIECES) - 1
+    seen_tab, opened = [], []
+    left_in_block = {b: sum(1 for j, p in enumerate(PIECES) if p[1] == b and j != last) for b in range(NB)}
+    v.wait_ge(S.xz, 2)
     v.wait_ge(S.xl, 16)
-    v.tensor_copy(T.xp[:, H:H + W], T.xs[:, :]).then_inc(S.xz, 1)
-    v.wait_ge(S.xz, 3)
-    for j, tab in enumerate(ORDER):
-        if j == 0:
-            v.wait_ge(S.c1, 16)
+    for j, (tab, b) in enumerate(PIECES):
+        if tab not in seen_tab:
+            seen_tab.append(tab)
+            v.wait_ge(S["tl%d" % tab], 16)
+        if j == 1:
+            v.wait_ge(S.xa, 1)
         if j == 2:
-            v.wait_ge(S.c2, 16)
-        v.tensor_tensor(T.pr[:, W * j:W * j + W], T.ts[:, OFF[tab]:OFF[tab] + W], T.xp[:, tab:tab + W],
+            v.wait_ge(S.xb, 1)
+        c0 = B * b
+        if j == 0:
+            xop = T.xs[:, c0:c0 + B]
+        else:
+            xop = T.xp[:, XO + c0 + tab - H:XO + c0 + tab - H + B]
+        v.tensor_tensor(T.pr[:, B * j:B * j + B], T.ts[:, W * tab + c0:W * tab + c0 + B], xop,
                         mult).then_inc(S["p%d" % j], 1)
-
-    te.wait_ge(S.idl, 16)
-    for j in range(KW - 1):
+        if j == last:
+            break
         te.wait_ge(S["p%d" % j], 1)
-        mm = te.matmul(T.acc[:, :], T.ident[:, :], T.pr[:, W * j:W * j + W], j == 0, j == KW - 2)
-    mm.then_inc(S.accd, 1)
+        left_in_block[b] -= 1
+        mm = te.matmul(T.acc[:, W * b:W * b + B], T.ident[:, :], T.pr[:, B * j:B * j + B],
+                       b not in opened, left_in_block[b] == 0)
+        opened.append(b)
+        if left_in_block[b] == 0:
+            mm.then_inc(S["a%d" % b], 1)
 
-    v.wait_ge(S.p4, 1)
-    v.wait_ge(S.accd, 1)
-    v.tensor_tensor(T.ys[:, :], T.acc[:, :], T.pr[:, W * (KW - 1):W * KW], add).then_inc(S.yadd, 1)
+    bl = NB - 1
+    v.wait_ge(S["p%d" % last], 1)
+    v.wait_ge(S["a%d" % bl], 1)
+    v.tensor_tensor(T.ys[:, B * bl:B * bl + B], T.acc[:, W * bl:W * bl + B], T.pr[:, B * last:B * last + B],
+                    add).then_inc(S.yadd, 1)
 
-    v.wait_ge(S.arrived, 2 * k)
-    a = OFF[4] + W - H
-    v.tensor_tensor(T.hp[:, :], T.ts[:, a:a + 2 * H], T.halo[:, :], mult).then_inc(S.h1, 1)
-    b0, b1 = OFF[3] + W - 1, OFF[1]
-    v.tensor_tensor(T.hq[:, :], T.ts[:, b0:b1 + 1:b1 - b0], T.halo[:, 0:2 * H:2 * H - 1], mult).then_inc(S.h1, 1)
-    v.wait_ge(S.h1, 2)
-    v.tensor_tensor(T.hp[:, 1:3], T.hp[:, 1:3], T.hq[:, :], add).then_inc(S.h2, 1)
-    v.wait_ge(S.h2, 1)
+    for b in range(NB - 1):
+        sc.wait_ge(S["a%d" % b], 1)
+        sc.activation(T.ys[:, B * b:B * b + B], T.acc[:, W * b:W * b + B], copy).then_inc(S["e%d" % b], 1)
+    sy.wait_ge(S.e0, 1)
+    sy.dma_start(T.y[:, H:B], T.ys[:, H:B]).then_inc(S.st, 16)
+    sy.wait_ge(S.e1, 1)
+    sy.wait_ge(S.e2, 1)
+    sy.dma_start(T.y[:, B:3 * B], T.ys[:, B:3 * B]).then_inc(S.st, 16)
+    sy.wait_ge(S.yadd, 1)
+    sy.dma_start(T.y[:, B * bl:W - H], T.ys[:, B * bl:W - H]).then_inc(S.st, 16)
+
+    def col(tab, c):
+        return T.ts[:, W * tab + c:W * tab + c + 1]
+
     v.wait_ge(S.yadd, 1)
-    v.tensor_tensor(T.ys[:, W - H:W], T.ys[:, W - H:W], T.hp[:, 0:H], add).then_inc(S.fin, 1)
-    v.tensor_tensor(T.ys[:, 0:H], T.ys[:, 0:H], T.hp[:, H:2 * H], add).then_inc(S.fin, 1)
+    v.wait_ge(S.arr_r, k)
+    v.tensor_scalar(T.qr[:, 0:1], col(3, W - 1), T.hr[:, 0:1], T.ys[:, W - 1:W], mult, add).then_inc(S.r1, 1)
+    v.tensor_scalar(T.yer[:, 0:1], col(4, W - 2), T.hr[:, 0:1], T.ys[:, W - 2:W - 1], mult, add).then_inc(S.fr, 1)
+    v.wait_ge(S.r1, 1)
+    v.tensor_scalar(T.yer[:, 1:2], col(4, W - 1), T.hr[:, 1:2], T.qr[:, 0:1], mult, add).then_inc(S.fr, 1)
+    sc.wait_ge(S.fr, 2)
+    sc.dma_start(T.y[:, W - H:W], T.yer[:, 0:H]).then_inc(S.st2, 16)
 
-    sy.wait_ge(S.fin, 2)
-    sy.dma_start(T.y[:, :], T.ys[:, :]).then_inc(S.st, 16)
-    sy.wait_ge(S.st, 16)
+    v.wait_ge(S.e0, 1)
+    v.wait_ge(S.arr_l, k)
+    v.tensor_scalar(T.ql[:, 0:1], col(1, 0), T.hl[:, 1:2], T.ys[:, 0:1], mult, add).then_inc(S.l1, 1)
+    v.tensor_scalar(T.yel[:, 1:2], col(0, 1), T.hl[:, 1:2], T.ys[:, 1:2], mult, add).then_inc(S.fl, 1)
+    v.wait_ge(S.l1, 1)
+    v.tensor_scalar(T.yel[:, 0:1], col(0, 0), T.hl[:, 0:1], T.ql[:, 0:1], mult, add).then_inc(S.fl, 1)
+    sy.wait_ge(S.fl, 2)
+    sy.dma_start(T.y[:, 0:H], T.yel[:, 0:H]).then_inc(S.st, 16)
+
+    sc.wait_ge(S.st2, 16)
+    sy.wait_ge(S.st, 64)

from concourse.bass import DstId, RemoteDMATransfer
from concourse.mybir import AluOpType, ActivationFunctionType

W = 512
KW = 5
H = 2
B = 128
NB = W // B
XO = 256
TABS = [2, 1, 3, 0, 4]
ENGINES_A_TRANSFER = 4
PIECES = [(tab, b) for tab in TABS for b in range(NB)]

SCRATCH = {
    "acc": ("psum", [128, NB * W], "float32"),
    "xp": ("psum", [128, 2 * W], "float32"),
    "xs": ("sbuf", [128, W], "bfloat16"),
    "ts": ("sbuf", [128, KW * W], "bfloat16"),
    "pr": ("sbuf", [128, KW * W], "bfloat16"),
    "ys": ("sbuf", [128, W], "bfloat16"),
    "el": ("sbuf", [128, 8], "bfloat16"),
    "er": ("sbuf", [128, 8], "bfloat16"),
    "hr": ("sbuf", [128, 8], "bfloat16"),
    "hl": ("sbuf", [128, 8], "bfloat16"),
    "qr": ("sbuf", [128, 8], "bfloat16"),
    "ql": ("sbuf", [128, 8], "bfloat16"),
    "yer": ("sbuf", [128, 8], "bfloat16"),
    "yel": ("sbuf", [128, 8], "bfloat16"),
    "ones": ("sbuf", [128, 128], "bfloat16"),
    "ident": ("sbuf", [128, 128], "bfloat16"),
}
SEMAPHORES = (["ea", "eb", "xl", "on", "xz", "idl", "xa", "xb", "arr_r", "arr_l", "sent", "yadd", "st", "st2",
               "r1", "l1", "fr", "fl"]
              + ["tl%d" % i for i in range(KW)] + ["p%d" % j for j in range(len(PIECES))]
              + ["a%d" % b for b in range(NB)] + ["e%d" % b for b in range(NB - 1)])


def _bits(mask):
    return [b for b in range(16) if (mask >> b) & 1]


def rank_program(g, core, T, topo):
    rank = T.rank_of(core)
    if rank is None:
        return
    n = len(T.cores)
    left, right = T.cores[(rank - 1) % n], T.cores[(rank + 1) % n]
    S = T.sem
    v, te, sy, sc = g.vector, g.tensor, g.sync, g.scalar
    mult, add = AluOpType.mult, AluOpType.add
    copy = ActivationFunctionType.Copy

    sy.dma_start(T.el[:, 0:H], T.x[:, 0:H]).then_inc(S.ea, 16)
    sy.dma_start(T.er[:, 0:H], T.x[:, W - H:W]).then_inc(S.eb, 16)
    sy.dma_start(T.xs[:, :], T.x[:, :]).then_inc(S.xl, 16)
    for tab in TABS:
        sy.dma_start(T.ts[:, W * tab:W * tab + W], T.t[:, W * tab:W * tab + W]).then_inc(S["tl%d" % tab], 16)

    v.memset(T.ones[:, :], 1.0).then_inc(S.on, 1)
    v.memset(T.xp[:, XO - H:XO], 0.0).then_inc(S.xz, 1)
    v.memset(T.xp[:, XO + W:XO + W + H], 0.0).then_inc(S.xz, 1)
    g.wait_ge(S.on, 1)
    g.affine_select(T.ident[:, :], T.ones[:, :], [[-1, 128]], AluOpType.is_equal, 0.0, 0, 1).then_inc(S.idl, 1)

    for dst in (left, right):
        if not topo.may_write(core, dst):
            raise ValueError("core %d may not write to core %d" % (core, dst))
    eng = [b for b in _bits(topo.mask(core, left)) if b in _bits(topo.mask(core, right))]
    k = ENGINES_A_TRANSFER
    m_l = sum(1 << b for b in eng[0:k])
    m_r = sum(1 << b for b in eng[k:2 * k])
    rid_l, pid_l = topo.addr(left)[0:2]
    rid_r, pid_r = topo.addr(right)[0:2]
    g.wait_ge(S.ea, 16)
    g.remote_dma_fused([
        RemoteDMATransfer(dst_ids=[DstId(rid=rid_l, pnc=pid_l)], dma_engine_mask=m_l, remote_sem=S.arr_r,
                          src=T.el[:, 0:H], dst=T.hr[:, 0:H]),
    ], local_sem=S.sent)
    g.wait_ge(S.eb, 16)
    g.remote_dma_fused([
        RemoteDMATransfer(dst_ids=[DstId(rid=rid_r, pnc=pid_r)], dma_engine_mask=m_r, remote_sem=S.arr_l,
                          src=T.er[:, 0:H], dst=T.hl[:, 0:H]),
    ], local_sem=S.sent)
    g.wait_ge(S.sent, 2 * k)

    te.wait_ge(S.idl, 1)
    te.wait_ge(S.xz, 2)
    te.wait_ge(S.xl, 16)
    te.matmul(T.xp[:, XO:XO + W // 2], T.ident[:, :], T.xs[:, 0:W // 2], True, True).then_inc(S.xa, 1)
    sc.wait_ge(S.xz, 2)
    sc.wait_ge(S.xl, 16)
    sc.activation(T.xp[:, XO + W // 2:XO + W], T.xs[:, W // 2:W], copy).then_inc(S.xb, 1)

    last = len(PIECES) - 1
    seen_tab, opened = [], []
    left_in_block = {b: sum(1 for j, p in enumerate(PIECES) if p[1] == b and j != last) for b in range(NB)}
    v.wait_ge(S.xz, 2)
    v.wait_ge(S.xl, 16)
    for j, (tab, b) in enumerate(PIECES):
        if tab not in seen_tab:
            seen_tab.append(tab)
            v.wait_ge(S["tl%d" % tab], 16)
        if j == 1:
            v.wait_ge(S.xa, 1)
        if j == 2:
            v.wait_ge(S.xb, 1)
        c0 = B * b
        if j == 0:
            xop = T.xs[:, c0:c0 + B]
        else:
            xop = T.xp[:, XO + c0 + tab - H:XO + c0 + tab - H + B]
        v.tensor_tensor(T.pr[:, B * j:B * j + B], T.ts[:, W * tab + c0:W * tab + c0 + B], xop,
                        mult).then_inc(S["p%d" % j], 1)
        if j == last:
            break
        te.wait_ge(S["p%d" % j], 1)
        left_in_block[b] -= 1
        mm = te.matmul(T.acc[:, W * b:W * b + B], T.ident[:, :], T.pr[:, B * j:B * j + B],
                       b not in opened, left_in_block[b] == 0)
        opened.append(b)
        if left_in_block[b] == 0:
            mm.then_inc(S["a%d" % b], 1)

    bl = NB - 1
    v.wait_ge(S["p%d" % last], 1)
    v.wait_ge(S["a%d" % bl], 1)
    v.tensor_tensor(T.ys[:, B * bl:B * bl + B], T.acc[:, W * bl:W * bl + B], T.pr[:, B * last:B * last + B],
                    add).then_inc(S.yadd, 1)

    for b in range(NB - 1):
        sc.wait_ge(S["a%d" % b], 1)
        sc.activation(T.ys[:, B * b:B * b + B], T.acc[:, W * b:W * b + B], copy).then_inc(S["e%d" % b], 1)
    sy.wait_ge(S.e0, 1)
    sy.dma_start(T.y[:, H:B], T.ys[:, H:B]).then_inc(S.st, 16)
    sy.wait_ge(S.e1, 1)
    sy.wait_ge(S.e2, 1)
    sy.dma_start(T.y[:, B:3 * B], T.ys[:, B:3 * B]).then_inc(S.st, 16)
    sy.wait_ge(S.yadd, 1)
    sy.dma_start(T.y[:, B * bl:W - H], T.ys[:, B * bl:W - H]).then_inc(S.st, 16)

    def col(tab, c):
        return T.ts[:, W * tab + c:W * tab + c + 1]

    v.wait_ge(S.yadd, 1)
    v.wait_ge(S.arr_r, k)
    v.tensor_scalar(T.qr[:, 0:1], col(3, W - 1), T.hr[:, 0:1], T.ys[:, W - 1:W], mult, add).then_inc(S.r1, 1)
    v.tensor_scalar(T.yer[:, 0:1], col(4, W - 2), T.hr[:, 0:1], T.ys[:, W - 2:W - 1], mult, add).then_inc(S.fr, 1)
    v.wait_ge(S.r1, 1)
    v.tensor_scalar(T.yer[:, 1:2], col(4, W - 1), T.hr[:, 1:2], T.qr[:, 0:1], mult, add).then_inc(S.fr, 1)
    sc.wait_ge(S.fr, 2)
    sc.dma_start(T.y[:, W - H:W], T.yer[:, 0:H]).then_inc(S.st2, 16)

    v.wait_ge(S.e0, 1)
    v.wait_ge(S.arr_l, k)
    v.tensor_scalar(T.ql[:, 0:1], col(1, 0), T.hl[:, 1:2], T.ys[:, 0:1], mult, add).then_inc(S.l1, 1)
    v.tensor_scalar(T.yel[:, 1:2], col(0, 1), T.hl[:, 1:2], T.ys[:, 1:2], mult, add).then_inc(S.fl, 1)
    v.wait_ge(S.l1, 1)
    v.tensor_scalar(T.yel[:, 0:1], col(0, 0), T.hl[:, 0:1], T.ql[:, 0:1], mult, add).then_inc(S.fl, 1)
    sy.wait_ge(S.fl, 2)
    sy.dma_start(T.y[:, 0:H], T.yel[:, 0:H]).then_inc(S.st, 16)

    sc.wait_ge(S.st2, 16)
    sy.wait_ge(S.st, 64)
